import numpy as np
import ml_dtypes


def mxq(x, axis, fmt="e4m3"):
    dtype, down = {"e4m3": (ml_dtypes.float8_e4m3fn, 7), "e5m2": (ml_dtypes.float8_e5m2, 14)}[fmt]
    v = np.moveaxis(np.asarray(x, np.float32).astype(ml_dtypes.bfloat16).astype(np.float64), axis, -1)
    blocks = v.reshape(v.shape[:-1] + (-1, 32))
    amax = np.abs(blocks).max(-1, keepdims=True)
    byte = np.maximum(np.where(amax > 0, np.frexp(amax)[1] - 1 + 127, 0) - down, 1)
    scale = np.exp2(byte - 127.0)
    codes = (blocks / scale).astype(np.float32).astype(dtype).astype(np.float64)
    return np.moveaxis((codes * scale).reshape(v.shape), -1, axis)


WIDE = False


def mx_kscale(k, group=512):
    if not WIDE:
        return np.ones(k)
    levels = np.array([10, -10, 5, -5, 0])
    if group != 512:
        return np.exp2(np.random.permutation(np.resize(levels, k // group))).repeat(group)
    if k % 512:
        return np.exp2(np.random.permutation(np.resize(levels, k // 32))).repeat(32)
    a = np.empty((k // 512, 16))
    for p in range(k // 512):
        a[p, :8] = np.random.permutation(np.resize(levels, 8))
        for g in range(8):
            far = levels[np.abs(levels - a[p, g]) >= 10]
            a[p, g + 8] = far[np.random.randint(len(far))]
    return np.exp2(a.ravel()).repeat(32)


def f64(x):
    return np.asarray(x).astype(np.float64)


def striped(idx):
    return np.tile(np.asarray(idx).reshape(-1, 16).T, (8, 1)).astype(np.uint16)


def unstriped(offs):
    return offs[:16].T.reshape(-1).astype(np.int64)


H, KV, D, NQ, N = 8, 2, 128, 512, 512


def setup_inputs():
    n = np.random.standard_normal
    s = mx_kscale(D, 0)[:, None]
    u = mx_kscale(N)
    t = np.random.uniform(0.5, 2.0, N) * u
    v = n((KV, N, 128))
    return {
        "qT": (n((H, D, NQ)) * s * (0.70 / np.sqrt(D))).astype(np.float32),
        "kT": (n((KV, D, N)) / s).astype(np.float32),
        "t": t.reshape(N, 1).astype(np.float32),
        "v": (v / t[:, None]).astype(np.float32),
        "gn": np.tile(np.random.uniform(0.5, 2.0, 128), (128, 1)).astype(np.float32),
        "og": n((H, NQ, 128)).astype(np.float32),
    }


def reference(qT, kT, t, v, gn, og):
    a = np.repeat(mxq(f64(kT), 1, "e4m3"), H // KV, 0).transpose(0, 2, 1) @ mxq(f64(qT), 1, "e4m3")
    p = a / (1.0 + np.exp(-a))
    w = p * f64(t)
    y = mxq(w, 1, "e4m3").transpose(0, 2, 1) @ np.repeat(mxq(f64(v), 1, "e4m3"), H // KV, 0)
    y = y / 16.0
    y = y / np.sqrt(np.mean(np.square(y), -1, keepdims=True) + 1e-5) * f64(gn)[:1]
    y = y / (1.0 + np.exp(-f64(og)))
    return y

@@ -1,0 +1,305 @@
+from contextlib import ExitStack
+
+import concourse.mybir as mybir
+
+H, KV, D, NQ, N = 8, 2, 128, 512, 512
+FLOPS = 2 * 2 * H * D * NQ * N
+
+F32 = mybir.dt.float32
+BF16 = mybir.dt.bfloat16
+U32 = mybir.dt.uint32
+U8 = mybir.dt.uint8
+FP8X4 = mybir.dt.float8_e4m3fn_x4
+ACT = mybir.ActivationFunctionType
+ALU = mybir.AluOpType
+
+P = 128
+PACK = 4
+ROWS = 32
+TILES = 4
+QC = 128
+CHUNKS = NQ // QC
+SETS = H // TILES
+GROUPS = SETS * CHUNKS
+GW = TILES * QC
+K_SPLIT = 88
+P_BUFS = 3
+
+
+def tile_rows_a_silu_onorm_gate_kernel(tc, qT, kT, t, v, gn, og, out):
+    nc = tc.nc
+
+    with ExitStack() as ctx:
+        sb = ctx.enter_context(tc.tile_pool(name="sb", bufs=1))
+        ps = ctx.enter_context(tc.psum_pool(name="ps", bufs=1))
+        ctx.enter_context(tc.manual_schedule())
+
+        q_raw = sb.tile([P, SETS, PACK, NQ], F32, name="q_raw", align_bytes=64)
+        q_bf = sb.tile([P, SETS * NQ * PACK], BF16, name="q_bf", align_bytes=64)
+        q_codes = sb.tile([P, SETS * NQ], U32, name="q_codes", align_bytes=64)
+        q_scales = sb.tile([P, SETS * NQ], U8, name="q_scales", align_bytes=64)
+        k_raw = sb.tile([P, PACK, N], F32, name="k_raw", align_bytes=64)
+        k_bf = sb.tile([P, N * PACK], BF16, name="k_bf", align_bytes=64)
+        k_codes = sb.tile([P, N], U32, name="k_codes", align_bytes=64)
+        k_scales = sb.tile([P, N], U8, name="k_scales", align_bytes=64)
+        v_raw = sb.tile([P, KV, PACK, D], F32, name="v_raw", align_bytes=64)
+        v_bf = sb.tile([P, KV * D * PACK], BF16, name="v_bf", align_bytes=64)
+        v_codes = sb.tile([P, KV * D], U32, name="v_codes", align_bytes=64)
+        v_scales = sb.tile([P, KV * D], U8, name="v_scales", align_bytes=64)
+        t_sb = sb.tile([P, PACK], F32, name="t_sb", align_bytes=64)
+        gn_sb = sb.tile([P, D], F32, name="gn_sb", align_bytes=64)
+        og_sb = sb.tile([P, H, CHUNKS, D], F32, name="og_sb", align_bytes=64)
+        gate = sb.tile([P, GROUPS, GW], F32, name="gate", align_bytes=64)
+        p_sb = sb.tile([P, P_BUFS, GW * PACK], F32, name="p_sb", align_bytes=64)
+        w_bf = sb.tile([P, GROUPS, GW * PACK], BF16, name="w_bf", align_bytes=64)
+        w_codes = sb.tile([P, GROUPS, GW], U32, name="w_codes", align_bytes=64)
+        w_scales = sb.tile([P, GROUPS, GW], U8, name="w_scales", align_bytes=64)
+        squares = sb.tile([P, GROUPS, GW], BF16, name="squares", align_bytes=64)
+        sums = sb.tile([P, GROUPS, 8], F32, name="sums", align_bytes=64)
+        means = sb.tile([P, GROUPS, 8], F32, name="means", align_bytes=64)
+        rstd = sb.tile([P, GROUPS, 8], F32, name="rstd", align_bytes=64)
+        expo = sb.tile([P, 8], F32, name="expo", align_bytes=64)
+        warm = sb.tile([P, 8], F32, name="warm", align_bytes=64)
+        res = sb.tile([P, GROUPS, GW], F32, name="res", align_bytes=64)
+        s_bank = [ps.tile([P, PACK * QC], F32, name="s_bank%d" % g) for g in range(TILES)]
+        y_bank = [ps.tile([P, GW], F32, name="y_bank%d" % b) for b in range(4)]
+
+        def load_q(s, c0, c1):
+            for half in range(2):
+                h0 = 4 * half + 2 * s
+                nc.sync.dma_start(
+                    out=q_raw[64 * half : 64 * half + 64, s, :, c0 * QC : c1 * QC],
+                    in_=qT[h0 : h0 + 2, :, c0 * QC : c1 * QC].rearrange("h (p j) q -> (h p) j q", j=PACK),
+                )
+
+        def load_og(h0):
+            nc.sync.dma_start(
+                out=og_sb[:, h0 : h0 + 2, :, :].rearrange("p h c e -> p (h c) e"),
+                in_=og[h0 : h0 + 2].rearrange("h (c p) e -> p (h c) e", p=P),
+            )
+
+        def cast(eng, dst, src):
+            if eng == "v":
+                nc.vector.tensor_copy(out=dst, in_=src)
+            else:
+                nc.scalar.copy(out=dst, in_=src)
+
+        def cast_q(eng, s, c0, c1):
+            lo, hi = (s * NQ + c0 * QC) * PACK, (s * NQ + c1 * QC) * PACK
+            cast(
+                eng,
+                q_bf[:, lo:hi].rearrange("p (c i j) -> p c j i", i=4, j=PACK),
+                q_raw[:, s, :, c0 * QC : c1 * QC].rearrange("p j (c i) -> p c j i", i=4),
+            )
+
+        def quant_q(s, c0, c1):
+            lo, hi = s * NQ + c0 * QC, s * NQ + c1 * QC
+            nc.vector.quantize_mx(
+                out=q_codes[:, lo:hi].bitcast(FP8X4),
+                scales=q_scales[:, lo:hi],
+                in_=q_bf[:, lo * PACK : hi * PACK],
+            )
+
+        def cast_k(eng, s0, s1):
+            cast(
+                eng,
+                k_bf[:].rearrange("p (r s j) -> p s j r", r=PACK, j=PACK)[:, s0:s1, :, :],
+                k_raw[:].rearrange("p j (s r) -> p s j r", r=PACK)[:, s0:s1, :, :],
+            )
+
+        def scores(n):
+            s, c = divmod(n, CHUNKS)
+            cols = slice(s * NQ + c * QC, s * NQ + (c + 1) * QC)
+            for g in range(TILES):
+                rows = slice(ROWS * g, ROWS * (g + 1))
+                for r in range(PACK):
+                    keys = slice(r * P, (r + 1) * P)
+                    nc.tensor.matmul_mx(
+                        out=s_bank[g][:, r * QC : (r + 1) * QC],
+                        lhsT=k_codes[rows, keys].bitcast(FP8X4),
+                        lhsT_scale=k_scales[rows, keys],
+                        rhs=q_codes[rows, cols].bitcast(FP8X4),
+                        rhs_scale=q_scales[rows, cols],
+                        start=True,
+                        stop=True,
+                    )
+
+        def silu(n):
+            for g in range(TILES):
+                nc.scalar.activation(
+                    out=p_sb[:, n % P_BUFS, g * QC * PACK : (g + 1) * QC * PACK].rearrange("p (q r) -> p q r", r=PACK),
+                    in_=s_bank[g][:].rearrange("p (r q) -> p q r", r=PACK),
+                    func=ACT.Silu,
+                )
+
+        def weigh(n, g0, g1):
+            lo, hi = g0 * QC * PACK, g1 * QC * PACK
+            nc.vector.tensor_tensor(
+                out=w_bf[:, n, lo:hi].rearrange("p (q r) -> p q r", r=PACK),
+                in0=p_sb[:, n % P_BUFS, lo:hi].rearrange("p (q r) -> p q r", r=PACK),
+                in1=t_sb[:].unsqueeze(1).to_broadcast([P, (g1 - g0) * QC, PACK]),
+                op=ALU.mult,
+            )
+
+        def quant_w(n, g0, g1):
+            nc.vector.quantize_mx(
+                out=w_codes[:, n, g0 * QC : g1 * QC].bitcast(FP8X4),
+                scales=w_scales[:, n, g0 * QC : g1 * QC],
+                in_=w_bf[:, n, g0 * QC * PACK : g1 * QC * PACK],
+            )
+
+        def y_of(n, g):
+            last_half = n == GROUPS - 1 and g >= 2
+            return y_bank[(n + 1) % 4 if last_half else n % 4][:, g * D : (g + 1) * D]
+
+        def values(n, g0, g1):
+            for g in range(g0, g1):
+                cols = slice(g * QC, (g + 1) * QC)
+                feats = slice((g // 2) * D, (g // 2 + 1) * D)
+                nc.tensor.matmul_mx(
+                    out=y_of(n, g),
+                    lhsT=w_codes[:, n, cols].bitcast(FP8X4),
+                    lhsT_scale=w_scales[:, n, cols],
+                    rhs=v_codes[:, feats].bitcast(FP8X4),
+                    rhs_scale=v_scales[:, feats],
+                    start=True,
+                    stop=True,
+                )
+
+        def square(n, g0, g1):
+            for g in range(g0, g1):
+                nc.scalar.activation(
+                    out=squares[:, n, g * D : (g + 1) * D],
+                    in_=y_of(n, g),
+                    func=ACT.Square,
+                    accum_out=sums[:, n, g : g + 1],
+                )
+
+        def norm(n, g0, g1):
+            nc.vector.tensor_scalar(
+                out=means[:, n, g0:g1],
+                in0=sums[:, n, g0:g1],
+                scalar1=4.0 / D,
+                scalar2=4.0 * 256.0 * 1e-5,
+                op0=ALU.mult,
+                op1=ALU.add,
+            )
+            nc.gpsimd.tensor_tensor(out=rstd[:, n, g0:g1], in0=means[:, n, g0:g1], in1=expo[:, g0:g1], op=ALU.pow)
+
+        def tanh(n):
+            s, c = divmod(n, CHUNKS)
+            nc.scalar.activation(
+                out=gate[:, n, :].rearrange("p (a b e) -> p a b e", a=2, b=2),
+                in_=og_sb[:].rearrange("p (a s b) c e -> p a s b c e", a=2, s=2)[:, :, s, :, c, :],
+                func=ACT.Tanh,
+                scale=0.5,
+            )
+
+        def gain(n):
+            view = gate[:, n, :].rearrange("p (g e) -> p g e", g=TILES)
+            nc.vector.scalar_tensor_tensor(
+                out=view,
+                in0=view,
+                scalar=1.0,
+                in1=gn_sb[:].unsqueeze(1).to_broadcast([P, TILES, D]),
+                op0=ALU.add,
+                op1=ALU.mult,
+            )
+
+        def finish(n, g0, g1):
+            s, c = divmod(n, CHUNKS)
+            for g in range(g0, g1):
+                cols = slice(g * D, (g + 1) * D)
+                nc.vector.scalar_tensor_tensor(
+                    out=res[:, n, cols],
+                    in0=y_of(n, g),
+                    scalar=rstd[:, n, g : g + 1],
+                    in1=gate[:, n, cols],
+                    op0=ALU.mult,
+                    op1=ALU.mult,
+                )
+                if g % 2 == 1:
+                    h0 = 4 * (g // 2) + 2 * s
+                    nc.sync.dma_start(
+                        out=out[h0 : h0 + 2, c * QC : (c + 1) * QC, :].rearrange("h q e -> q h e"),
+                        in_=res[:, n, (g - 1) * D : (g + 1) * D].rearrange("p (h e) -> p h e", h=2),
+                    )
+
+        load_q(0, 0, 1)
+        for g in (0, 2, 1, 3):
+            nc.sync.dma_start(
+                out=k_raw[ROWS * g : ROWS * (g + 1), :, :],
+                in_=kT[g // 2].rearrange("(p j) n -> p j n", j=PACK),
+            )
+        nc.sync.dma_start(out=t_sb[:], in_=t.rearrange("(p j) o -> p (j o)", j=PACK))
+        load_q(0, 1, 2)
+        nc.sync.dma_start(
+            out=v_raw[:].rearrange("p k j e -> p k (j e)"),
+            in_=v.rearrange("k (p j) e -> p k (j e)", j=PACK),
+        )
+        load_q(0, 2, 4)
+        nc.sync.dma_start(out=gn_sb[:], in_=gn)
+        load_og(0)
+        load_og(4)
+        load_q(1, 0, 4)
+        load_og(2)
+        load_og(6)
+
+        nc.gpsimd.memset(expo[:], -0.5)
+        nc.scalar.activation(out=warm[:], in_=expo[:], func=ACT.Silu)
+
+        cast_q("v", 0, 0, 1)
+        quant_q(0, 0, 1)
+        cast_k("v", 0, K_SPLIT)
+        cast_k("s", K_SPLIT, P)
+        nc.vector.quantize_mx(out=k_codes[:].bitcast(FP8X4), scales=k_scales[:], in_=k_bf[:])
+        cast_q("s", 0, 1, 2)
+        scores(0)
+        quant_q(0, 1, 2)
+        for k in range(KV):
+            nc.vector.tensor_copy(
+                out=v_bf[:, k * D * PACK : (k + 1) * D * PACK].rearrange("p (c i j) -> p c j i", i=4, j=PACK),
+                in_=v_raw[:, k, :, :].rearrange("p j (c i) -> p c j i", i=4),
+            )
+
+        q_casts = {0: (0, 2, 4), 2: (1, 0, 2), 4: (1, 2, 4)}
+        tanhs = {1: (0, 1), 2: (2,), 3: (3, 4), 4: (5,), 5: (6,), 6: (7,)}
+        gains = {1: (0, 1), 2: (2,), 3: (3,), 4: (4,), 5: (5, 6), 6: (7,)}
+        last = GROUPS - 1
+        for n in range(GROUPS):
+            silu(n)
+            if n < last:
+                scores(n + 1)
+            if n >= 1:
+                square(n - 1, 0, TILES)
+            if n in q_casts:
+                cast_q("s", *q_casts[n])
+            for m in tanhs.get(n, ()):
+                tanh(m)
+            weigh(n, 0, 2)
+            if n == 0:
+                nc.vector.quantize_mx(out=v_codes[:].bitcast(FP8X4), scales=v_scales[:], in_=v_bf[:])
+            weigh(n, 2, 4)
+            if n < last:
+                if n >= 1:
+                    norm(n - 1, 0, TILES)
+                if n >= 2:
+                    finish(n - 2, 0, TILES)
+                for m in gains.get(n, ()):
+                    gain(m)
+                if n in q_casts:
+                    quant_q(*q_casts[n])
+                quant_w(n, 0, TILES)
+                values(n, 0, TILES)
+        quant_w(last, 0, 2)
+        values(last, 0, 2)
+        norm(last - 1, 0, TILES)
+        quant_w(last, 2, 4)
+        finish(last - 2, 0, TILES)
+        values(last, 2, 4)
+        square(last, 0, 2)
+        square(last, 2, 4)
+        norm(last, 0, 2)
+        finish(last - 1, 0, TILES)
+        norm(last, 2, 4)
+        finish(last, 0, TILES)

@@ -9,25 +9,38 @@ F32 = mybir.dt.float32
 BF16 = mybir.dt.bfloat16
 U32 = mybir.dt.uint32
 U8 = mybir.dt.uint8
+I32 = mybir.dt.int32
 FP8X4 = mybir.dt.float8_e4m3fn_x4
 ACT = mybir.ActivationFunctionType
 ALU = mybir.AluOpType
 
 P = 128
 PACK = 4
-ROWS = 32
-TILES = 4
+ROWS = D // PACK
+TILES = P // ROWS
+HALF = TILES // 2
 QC = 128
 CHUNKS = NQ // QC
 SETS = H // TILES
 GROUPS = SETS * CHUNKS
+LAST = GROUPS - 1
 GW = TILES * QC
-K_SPLIT = 88
-P_BUFS = 3
+LINE = 4
+P_BUFS = 4
+Y_BANKS = 4
+HEADS = ((2, 3, 4, 5), (0, 1, 6, 7))
+RUNS = (((0, TILES),), ((0, HALF), (HALF, TILES)))
+K_HALF, K_SHARE = P // 2, 3 * P // 4
+EPS = 256.0 * 1e-5
+FOLD = 4.0
+EARLY = 3
+SEED = float(0x5F3759DF)
+KAPPA = 8.0 / 3.0
 
 
 def tile_rows_a_silu_onorm_gate_kernel(tc, qT, kT, t, v, gn, og, out):
     nc = tc.nc
+    on_vector, on_scalar = nc.vector.tensor_copy, nc.scalar.copy
 
     with ExitStack() as ctx:
         sb = ctx.enter_context(tc.tile_pool(name="sb", bufs=1))
@@ -47,6 +60,7 @@ def tile_rows_a_silu_onorm_gate_kernel(tc, qT, kT, t, v, gn, og, out):
         v_codes = sb.tile([P, KV * D], U32, name="v_codes", align_bytes=64)
         v_scales = sb.tile([P, KV * D], U8, name="v_scales", align_bytes=64)
         t_sb = sb.tile([P, PACK], F32, name="t_sb", align_bytes=64)
+        t_wide = sb.tile([P, QC * PACK], F32, name="t_wide", align_bytes=64)
         gn_sb = sb.tile([P, D], F32, name="gn_sb", align_bytes=64)
         og_sb = sb.tile([P, H, CHUNKS, D], F32, name="og_sb", align_bytes=64)
         gate = sb.tile([P, GROUPS, GW], F32, name="gate", align_bytes=64)
@@ -55,61 +69,60 @@ def tile_rows_a_silu_onorm_gate_kernel(tc, qT, kT, t, v, gn, og, out):
         w_codes = sb.tile([P, GROUPS, GW], U32, name="w_codes", align_bytes=64)
         w_scales = sb.tile([P, GROUPS, GW], U8, name="w_scales", align_bytes=64)
         squares = sb.tile([P, GROUPS, GW], BF16, name="squares", align_bytes=64)
-        sums = sb.tile([P, GROUPS, 8], F32, name="sums", align_bytes=64)
-        means = sb.tile([P, GROUPS, 8], F32, name="means", align_bytes=64)
-        rstd = sb.tile([P, GROUPS, 8], F32, name="rstd", align_bytes=64)
-        expo = sb.tile([P, 8], F32, name="expo", align_bytes=64)
-        warm = sb.tile([P, 8], F32, name="warm", align_bytes=64)
+        sums = sb.tile([P, GROUPS * TILES], F32, name="sums", align_bytes=64)
+        factor = sb.tile([P, GROUPS * TILES], F32, name="factor", align_bytes=64)
+        steps = sb.tile([P, 9, 16], F32, name="steps", align_bytes=64)
+        warm = sb.tile([P, 2, 8], F32, name="warm", align_bytes=64)
         res = sb.tile([P, GROUPS, GW], F32, name="res", align_bytes=64)
         s_bank = [ps.tile([P, PACK * QC], F32, name="s_bank%d" % g) for g in range(TILES)]
-        y_bank = [ps.tile([P, GW], F32, name="y_bank%d" % b) for b in range(4)]
+        y_bank = [ps.tile([P, GW], F32, name="y_bank%d" % b) for b in range(Y_BANKS)]
 
-        def load_q(s, c0, c1):
-            for half in range(2):
-                h0 = 4 * half + 2 * s
+        def load_k(i0, i1):
+            both = kT.rearrange("k (p j) i -> (k p) j i", j=PACK)
+            nc.sync.dma_start(out=k_raw[ROWS : 3 * ROWS, :, i0:i1], in_=both[:, :, i0:i1])
+            nc.sync.dma_start(out=k_raw[0:ROWS, :, i0:i1], in_=both[0:ROWS, :, i0:i1])
+            nc.scalar.dma_start(out=k_raw[3 * ROWS : P, :, i0:i1], in_=both[ROWS : 2 * ROWS, :, i0:i1])
+
+        def load_q(hs, c0, c1):
+            for g0, g1 in RUNS[hs]:
+                h0 = HEADS[hs][g0]
                 nc.sync.dma_start(
-                    out=q_raw[64 * half : 64 * half + 64, s, :, c0 * QC : c1 * QC],
-                    in_=qT[h0 : h0 + 2, :, c0 * QC : c1 * QC].rearrange("h (p j) q -> (h p) j q", j=PACK),
+                    out=q_raw[ROWS * g0 : ROWS * g1, hs, :, c0 * QC : c1 * QC],
+                    in_=qT[h0 : h0 + g1 - g0, :, c0 * QC : c1 * QC].rearrange("h (p j) q -> (h p) j q", j=PACK),
                 )
 
-        def load_og(h0):
-            nc.sync.dma_start(
-                out=og_sb[:, h0 : h0 + 2, :, :].rearrange("p h c e -> p (h c) e"),
-                in_=og[h0 : h0 + 2].rearrange("h (c p) e -> p (h c) e", p=P),
-            )
+        def load_og(hs):
+            for g0 in (0, HALF):
+                h0 = HEADS[hs][g0]
+                nc.sync.dma_start(
+                    out=og_sb[:, TILES * hs + g0 : TILES * hs + g0 + HALF, :, :].rearrange("p h c e -> p (h c) e"),
+                    in_=og[h0 : h0 + HALF].rearrange("h (c p) e -> p (h c) e", p=P),
+                )
 
-        def cast(eng, dst, src):
-            if eng == "v":
-                nc.vector.tensor_copy(out=dst, in_=src)
-            else:
-                nc.scalar.copy(out=dst, in_=src)
-
-        def cast_q(eng, s, c0, c1):
-            lo, hi = (s * NQ + c0 * QC) * PACK, (s * NQ + c1 * QC) * PACK
-            cast(
-                eng,
-                q_bf[:, lo:hi].rearrange("p (c i j) -> p c j i", i=4, j=PACK),
-                q_raw[:, s, :, c0 * QC : c1 * QC].rearrange("p j (c i) -> p c j i", i=4),
-            )
-
-        def quant_q(s, c0, c1):
-            lo, hi = s * NQ + c0 * QC, s * NQ + c1 * QC
+        def quantize(codes, scales, source, c0, c1):
             nc.vector.quantize_mx(
-                out=q_codes[:, lo:hi].bitcast(FP8X4),
-                scales=q_scales[:, lo:hi],
-                in_=q_bf[:, lo * PACK : hi * PACK],
+                out=codes[:, c0:c1].bitcast(FP8X4), scales=scales[:, c0:c1], in_=source[:, c0 * PACK : c1 * PACK]
             )
 
-        def cast_k(eng, s0, s1):
-            cast(
-                eng,
-                k_bf[:].rearrange("p (r s j) -> p s j r", r=PACK, j=PACK)[:, s0:s1, :, :],
-                k_raw[:].rearrange("p j (s r) -> p s j r", r=PACK)[:, s0:s1, :, :],
+        def cast_k(copy, s0, s1):
+            copy(
+                out=k_bf[:].rearrange("p (r s j) -> p s j r", r=PACK, j=PACK)[:, s0:s1, :, :],
+                in_=k_raw[:].rearrange("p j (s r) -> p s j r", r=PACK)[:, s0:s1, :, :],
             )
+
+        def cast_q(copy, hs, c0, c1):
+            lo, hi = (hs * NQ + c0 * QC) * PACK, (hs * NQ + c1 * QC) * PACK
+            copy(
+                out=q_bf[:, lo:hi].rearrange("p (m c j) -> p m j c", c=LINE, j=PACK),
+                in_=q_raw[:, hs, :, c0 * QC : c1 * QC].rearrange("p j (m c) -> p m j c", c=LINE),
+            )
+
+        def quantize_q(hs, c0, c1):
+            quantize(q_codes, q_scales, q_bf, hs * NQ + c0 * QC, hs * NQ + c1 * QC)
 
         def scores(n):
-            s, c = divmod(n, CHUNKS)
-            cols = slice(s * NQ + c * QC, s * NQ + (c + 1) * QC)
+            hs, c = divmod(n, CHUNKS)
+            cols = slice(hs * NQ + c * QC, hs * NQ + (c + 1) * QC)
             for g in range(TILES):
                 rows = slice(ROWS * g, ROWS * (g + 1))
                 for r in range(PACK):
@@ -124,38 +137,34 @@ def tile_rows_a_silu_onorm_gate_kernel(tc, qT, kT, t, v, gn, og, out):
                         stop=True,
                     )
 
-        def silu(n):
-            for g in range(TILES):
+        def silu(n, g0=0, g1=TILES):
+            for g in range(g0, g1):
                 nc.scalar.activation(
                     out=p_sb[:, n % P_BUFS, g * QC * PACK : (g + 1) * QC * PACK].rearrange("p (q r) -> p q r", r=PACK),
                     in_=s_bank[g][:].rearrange("p (r q) -> p q r", r=PACK),
                     func=ACT.Silu,
                 )
 
-        def weigh(n, g0, g1):
-            lo, hi = g0 * QC * PACK, g1 * QC * PACK
+        def weigh(n, half):
+            lo, hi = half * HALF * QC * PACK, (half + 1) * HALF * QC * PACK
             nc.vector.tensor_tensor(
-                out=w_bf[:, n, lo:hi].rearrange("p (q r) -> p q r", r=PACK),
-                in0=p_sb[:, n % P_BUFS, lo:hi].rearrange("p (q r) -> p q r", r=PACK),
-                in1=t_sb[:].unsqueeze(1).to_broadcast([P, (g1 - g0) * QC, PACK]),
+                out=w_bf[:, n, lo:hi].rearrange("p (g w) -> p g w", g=HALF),
+                in0=p_sb[:, n % P_BUFS, lo:hi].rearrange("p (g w) -> p g w", g=HALF),
+                in1=t_wide[:].unsqueeze(1).to_broadcast([P, HALF, QC * PACK]),
                 op=ALU.mult,
             )
 
-        def quant_w(n, g0, g1):
-            nc.vector.quantize_mx(
-                out=w_codes[:, n, g0 * QC : g1 * QC].bitcast(FP8X4),
-                scales=w_scales[:, n, g0 * QC : g1 * QC],
-                in_=w_bf[:, n, g0 * QC * PACK : g1 * QC * PACK],
-            )
+        def quantize_w(n, g0=0, g1=TILES):
+            quantize(w_codes[:, n, :], w_scales[:, n, :], w_bf[:, n, :], g0 * QC, g1 * QC)
 
         def y_of(n, g):
-            last_half = n == GROUPS - 1 and g >= 2
-            return y_bank[(n + 1) % 4 if last_half else n % 4][:, g * D : (g + 1) * D]
+            bank = n + 1 if n == LAST and g >= HALF else n
+            return y_bank[bank % Y_BANKS][:, g * D : (g + 1) * D]
 
-        def values(n, g0, g1):
+        def values(n, g0=0, g1=TILES):
             for g in range(g0, g1):
                 cols = slice(g * QC, (g + 1) * QC)
-                feats = slice((g // 2) * D, (g // 2 + 1) * D)
+                feats = slice((g // HALF) * D, (g // HALF + 1) * D)
                 nc.tensor.matmul_mx(
                     out=y_of(n, g),
                     lhsT=w_codes[:, n, cols].bitcast(FP8X4),
@@ -166,140 +175,221 @@ def tile_rows_a_silu_onorm_gate_kernel(tc, qT, kT, t, v, gn, og, out):
                     stop=True,
                 )
 
-        def square(n, g0, g1):
+        def square(n, g0=0, g1=TILES):
             for g in range(g0, g1):
                 nc.scalar.activation(
                     out=squares[:, n, g * D : (g + 1) * D],
                     in_=y_of(n, g),
                     func=ACT.Square,
-                    accum_out=sums[:, n, g : g + 1],
+                    accum_out=sums[:, n * TILES + g : n * TILES + g + 1],
                 )
 
-        def norm(n, g0, g1):
-            nc.vector.tensor_scalar(
-                out=means[:, n, g0:g1],
-                in0=sums[:, n, g0:g1],
-                scalar1=4.0 / D,
-                scalar2=4.0 * 256.0 * 1e-5,
-                op0=ALU.mult,
-                op1=ALU.add,
+        def root(c0, c1):
+            nc.scalar.activation(
+                out=factor[:, c0:c1], in_=sums[:, c0:c1], func=ACT.Abs_reciprocal_sqrt, scale=FOLD / D, bias=FOLD * EPS
             )
-            nc.gpsimd.tensor_tensor(out=rstd[:, n, g0:g1], in0=means[:, n, g0:g1], in1=expo[:, g0:g1], op=ALU.pow)
+
+        def refine(x, z, z_scale, scratch, dst):
+            xz, u, poly = scratch
+            return [
+                lambda: nc.vector.tensor_tensor(out=xz, in0=x, in1=z, op=ALU.mult),
+                lambda: nc.vector.scalar_tensor_tensor(
+                    out=u, in0=xz, scalar=1.0 / z_scale**2, in1=z, op0=ALU.mult, op1=ALU.mult
+                ),
+                lambda: nc.vector.scalar_tensor_tensor(
+                    out=poly, in0=u, scalar=-10.0 / 3.0, in1=u, op0=ALU.add, op1=ALU.mult
+                ),
+                lambda: nc.vector.scalar_tensor_tensor(out=dst, in0=poly, scalar=5.0, in1=z, op0=ALU.add, op1=ALU.mult),
+            ]
+
+        def early_factor_steps():
+            cols = slice(0, EARLY * TILES)
+            row = [steps[:, i, cols] for i in range(9)]
+            x, guess, better = row[0], row[1], row[5]
+            lift = FOLD * KAPPA**4
+            return [
+                lambda: nc.vector.tensor_scalar(
+                    out=x, in0=sums[:, cols], scalar1=lift / D, scalar2=lift * EPS, op0=ALU.mult, op1=ALU.add
+                ),
+                lambda: nc.vector.tensor_scalar(
+                    out=guess.bitcast(I32), in0=x.bitcast(I32), scalar1=-0.5, scalar2=SEED, op0=ALU.mult, op1=ALU.add
+                ),
+                *refine(x, guess, 1.0, row[2:5], better),
+                *refine(x, better, KAPPA, row[6:9], factor[:, cols]),
+            ]
 
         def tanh(n):
-            s, c = divmod(n, CHUNKS)
+            hs, c = divmod(n, CHUNKS)
             nc.scalar.activation(
-                out=gate[:, n, :].rearrange("p (a b e) -> p a b e", a=2, b=2),
-                in_=og_sb[:].rearrange("p (a s b) c e -> p a s b c e", a=2, s=2)[:, :, s, :, c, :],
+                out=gate[:, n : n + 2, :].rearrange("p c (g e) -> p c g e", g=TILES),
+                in_=og_sb[:, TILES * hs : TILES * (hs + 1), c : c + 2, :].rearrange("p g c e -> p c g e"),
                 func=ACT.Tanh,
                 scale=0.5,
             )
 
         def gain(n):
-            view = gate[:, n, :].rearrange("p (g e) -> p g e", g=TILES)
+            view = gate[:, n : n + 2, :].rearrange("p c (g e) -> p (c g) e", g=TILES)
             nc.vector.scalar_tensor_tensor(
                 out=view,
                 in0=view,
                 scalar=1.0,
-                in1=gn_sb[:].unsqueeze(1).to_broadcast([P, TILES, D]),
+                in1=gn_sb[:].unsqueeze(1).to_broadcast([P, 2 * TILES, D]),
                 op0=ALU.add,
                 op1=ALU.mult,
             )
 
-        def finish(n, g0, g1):
-            s, c = divmod(n, CHUNKS)
-            for g in range(g0, g1):
-                cols = slice(g * D, (g + 1) * D)
-                nc.vector.scalar_tensor_tensor(
-                    out=res[:, n, cols],
-                    in0=y_of(n, g),
-                    scalar=rstd[:, n, g : g + 1],
-                    in1=gate[:, n, cols],
-                    op0=ALU.mult,
-                    op1=ALU.mult,
-                )
-                if g % 2 == 1:
-                    h0 = 4 * (g // 2) + 2 * s
-                    nc.sync.dma_start(
-                        out=out[h0 : h0 + 2, c * QC : (c + 1) * QC, :].rearrange("h q e -> q h e"),
-                        in_=res[:, n, (g - 1) * D : (g + 1) * D].rearrange("p (h e) -> p h e", h=2),
+        def finish(n):
+            hs, c = divmod(n, CHUNKS)
+            for g0, g1 in RUNS[hs]:
+                for g in range(g0, g1):
+                    cols = slice(g * D, (g + 1) * D)
+                    nc.vector.scalar_tensor_tensor(
+                        out=res[:, n, cols],
+                        in0=y_of(n, g),
+                        scalar=factor[:, n * TILES + g : n * TILES + g + 1],
+                        in1=gate[:, n, cols],
+                        op0=ALU.mult,
+                        op1=ALU.mult,
                     )
+                h0 = HEADS[hs][g0]
+                nc.sync.dma_start(
+                    out=out[h0 : h0 + g1 - g0, c * QC : (c + 1) * QC, :].rearrange("h q e -> q h e"),
+                    in_=res[:, n, g0 * D : g1 * D].rearrange("p (h e) -> p h e", e=D),
+                )
 
+
+        load_k(0, N // 2)
+        load_k(N // 2, N)
         load_q(0, 0, 1)
-        for g in (0, 2, 1, 3):
-            nc.sync.dma_start(
-                out=k_raw[ROWS * g : ROWS * (g + 1), :, :],
-                in_=kT[g // 2].rearrange("(p j) n -> p j n", j=PACK),
-            )
-        nc.sync.dma_start(out=t_sb[:], in_=t.rearrange("(p j) o -> p (j o)", j=PACK))
+        nc.sync.dma_start(out=t_sb[:], in_=t.rearrange("(p r) o -> p (r o)", r=PACK))
+        nc.vector.memset(warm[:, 0, :], 0.0)
+        nc.scalar.activation(out=warm[:, 1, :], in_=warm[:, 0, :], func=ACT.Silu)
         load_q(0, 1, 2)
         nc.sync.dma_start(
-            out=v_raw[:].rearrange("p k j e -> p k (j e)"),
-            in_=v.rearrange("k (p j) e -> p k (j e)", j=PACK),
+            out=v_raw[:].rearrange("p k r e -> p k (r e)"), in_=v.rearrange("k (p r) e -> p k (r e)", r=PACK)
         )
-        load_q(0, 2, 4)
-        nc.sync.dma_start(out=gn_sb[:], in_=gn)
+        load_q(0, 2, CHUNKS)
+        load_q(1, 0, 2)
         load_og(0)
-        load_og(4)
-        load_q(1, 0, 4)
-        load_og(2)
-        load_og(6)
+        nc.sync.dma_start(out=gn_sb[:], in_=gn)
+        load_q(1, 2, CHUNKS)
+        load_og(1)
 
-        nc.gpsimd.memset(expo[:], -0.5)
-        nc.scalar.activation(out=warm[:], in_=expo[:], func=ACT.Silu)
-
-        cast_q("v", 0, 0, 1)
-        quant_q(0, 0, 1)
-        cast_k("v", 0, K_SPLIT)
-        cast_k("s", K_SPLIT, P)
-        nc.vector.quantize_mx(out=k_codes[:].bitcast(FP8X4), scales=k_scales[:], in_=k_bf[:])
-        cast_q("s", 0, 1, 2)
+        cast_k(on_vector, 0, K_HALF)
+        cast_k(on_vector, K_HALF, K_SHARE)
+        cast_k(on_scalar, K_SHARE, P)
+        cast_q(on_scalar, 0, 0, 1)
+        quantize(k_codes, k_scales, k_bf, 0, N // 2)
+        quantize_q(0, 0, 1)
+        quantize(k_codes, k_scales, k_bf, N // 2, N)
         scores(0)
-        quant_q(0, 1, 2)
+
+        cast_q(on_scalar, 0, 1, 2)
+        nc.vector.tensor_copy(
+            out=t_wide[:].rearrange("p (q r) -> p q r", r=PACK),
+            in_=t_sb[:].unsqueeze(1).to_broadcast([P, QC, PACK]),
+        )
+        quantize_q(0, 1, 2)
         for k in range(KV):
             nc.vector.tensor_copy(
-                out=v_bf[:, k * D * PACK : (k + 1) * D * PACK].rearrange("p (c i j) -> p c j i", i=4, j=PACK),
-                in_=v_raw[:, k, :, :].rearrange("p j (c i) -> p c j i", i=4),
+                out=v_bf[:, k * D * PACK : (k + 1) * D * PACK].rearrange("p (m c r) -> p m r c", c=LINE, r=PACK),
+                in_=v_raw[:, k, :, :].rearrange("p r (m c) -> p m r c", c=LINE),
             )
+        silu(0)
+        scores(1)
+        cast_q(on_vector, 0, 2, 3)
+        cast_q(on_scalar, 0, 3, CHUNKS)
+        weigh(0, 0)
+        quantize(v_codes, v_scales, v_bf, 0, KV * D)
+        quantize_q(0, 2, CHUNKS)
+        weigh(0, 1)
 
-        q_casts = {0: (0, 2, 4), 2: (1, 0, 2), 4: (1, 2, 4)}
-        tanhs = {1: (0, 1), 2: (2,), 3: (3, 4), 4: (5,), 5: (6,), 6: (7,)}
-        gains = {1: (0, 1), 2: (2,), 3: (3,), 4: (4,), 5: (5, 6), 6: (7,)}
-        last = GROUPS - 1
-        for n in range(GROUPS):
-            silu(n)
-            if n < last:
-                scores(n + 1)
-            if n >= 1:
-                square(n - 1, 0, TILES)
-            if n in q_casts:
-                cast_q("s", *q_casts[n])
-            for m in tanhs.get(n, ()):
-                tanh(m)
-            weigh(n, 0, 2)
-            if n == 0:
-                nc.vector.quantize_mx(out=v_codes[:].bitcast(FP8X4), scales=v_scales[:], in_=v_bf[:])
-            weigh(n, 2, 4)
-            if n < last:
-                if n >= 1:
-                    norm(n - 1, 0, TILES)
-                if n >= 2:
-                    finish(n - 2, 0, TILES)
-                for m in gains.get(n, ()):
-                    gain(m)
-                if n in q_casts:
-                    quant_q(*q_casts[n])
-                quant_w(n, 0, TILES)
-                values(n, 0, TILES)
-        quant_w(last, 0, 2)
-        values(last, 0, 2)
-        norm(last - 1, 0, TILES)
-        quant_w(last, 2, 4)
-        finish(last - 2, 0, TILES)
-        values(last, 2, 4)
-        square(last, 0, 2)
-        square(last, 2, 4)
-        norm(last, 0, 2)
-        finish(last - 1, 0, TILES)
-        norm(last, 2, 4)
-        finish(last, 0, TILES)
+        silu(1)
+        scores(2)
+        weigh(1, 0)
+        weigh(1, 1)
+        silu(2)
+        scores(3)
+        cast_q(on_scalar, 1, 0, 2)
+        quantize_w(0)
+        values(0)
+        weigh(2, 0)
+        quantize_w(1)
+        values(1)
+        weigh(2, 1)
+        quantize_q(1, 0, 2)
+        silu(3)
+        quantize_w(2)
+        scores(4)
+        values(2)
+        tanh(0)
+        for n in range(EARLY):
+            square(n)
+        weigh(3, 0)
+        weigh(3, 1)
+        gain(0)
+
+        silu(4, 0, HALF)
+        tanh(2)
+        silu(4, HALF, TILES)
+        scores(5)
+        cast_q(on_scalar, 1, 2, CHUNKS)
+        short = early_factor_steps()
+        short[0]()
+        between = [
+            lambda: quantize_w(3),
+            lambda: weigh(4, 0),
+            lambda: gain(2),
+            lambda: weigh(4, 1),
+            lambda: quantize_q(1, 2, CHUNKS),
+            lambda: quantize_w(4),
+        ]
+        for step, longer in zip(short[1:], between):
+            step()
+            longer()
+        short[7]()
+        silu(5)
+        scores(6)
+        silu(6)
+        scores(LAST)
+        values(3)
+        silu(LAST)
+        tanh(4)
+        tanh(6)
+        for half in range(2):
+            weigh(5, half)
+            short[8 + half]()
+
+        weigh(6, 0)
+        quantize_w(5)
+        weigh(6, 1)
+        finish(0)
+        values(4)
+        finish(1)
+        values(5)
+        finish(2)
+        quantize_w(6)
+        values(6)
+        weigh(LAST, 0)
+        weigh(LAST, 1)
+        gain(4)
+
+        for n in (3, 4):
+            square(n)
+            root(n * TILES, (n + 1) * TILES)
+        square(5)
+        square(6)
+        root(5 * TILES, 6 * TILES)
+        quantize_w(LAST, 0, HALF)
+        finish(3)
+        values(LAST, 0, HALF)
+        quantize_w(LAST, HALF, TILES)
+        finish(4)
+        values(LAST, HALF, TILES)
+        square(LAST, 0, HALF)
+        root(6 * TILES, LAST * TILES + HALF)
+        square(LAST, HALF, TILES)
+        root(LAST * TILES + HALF, GROUPS * TILES)
+        gain(6)
+        for n in (5, 6, LAST):
+            finish(n)

from contextlib import ExitStack

import concourse.mybir as mybir

H, KV, D, NQ, N = 8, 2, 128, 512, 512
FLOPS = 2 * 2 * H * D * NQ * N

F32 = mybir.dt.float32
BF16 = mybir.dt.bfloat16
U32 = mybir.dt.uint32
U8 = mybir.dt.uint8
I32 = mybir.dt.int32
FP8X4 = mybir.dt.float8_e4m3fn_x4
ACT = mybir.ActivationFunctionType
ALU = mybir.AluOpType

P = 128
PACK = 4
ROWS = D // PACK
TILES = P // ROWS
HALF = TILES // 2
QC = 128
CHUNKS = NQ // QC
SETS = H // TILES
GROUPS = SETS * CHUNKS
LAST = GROUPS - 1
GW = TILES * QC
LINE = 4
P_BUFS = 4
Y_BANKS = 4
HEADS = ((2, 3, 4, 5), (0, 1, 6, 7))
RUNS = (((0, TILES),), ((0, HALF), (HALF, TILES)))
K_HALF, K_SHARE = P // 2, 3 * P // 4
EPS = 256.0 * 1e-5
FOLD = 4.0
EARLY = 3
SEED = float(0x5F3759DF)
KAPPA = 8.0 / 3.0


def tile_rows_a_silu_onorm_gate_kernel(tc, qT, kT, t, v, gn, og, out):
    nc = tc.nc
    on_vector, on_scalar = nc.vector.tensor_copy, nc.scalar.copy

    with ExitStack() as ctx:
        sb = ctx.enter_context(tc.tile_pool(name="sb", bufs=1))
        ps = ctx.enter_context(tc.psum_pool(name="ps", bufs=1))
        ctx.enter_context(tc.manual_schedule())

        q_raw = sb.tile([P, SETS, PACK, NQ], F32, name="q_raw", align_bytes=64)
        q_bf = sb.tile([P, SETS * NQ * PACK], BF16, name="q_bf", align_bytes=64)
        q_codes = sb.tile([P, SETS * NQ], U32, name="q_codes", align_bytes=64)
        q_scales = sb.tile([P, SETS * NQ], U8, name="q_scales", align_bytes=64)
        k_raw = sb.tile([P, PACK, N], F32, name="k_raw", align_bytes=64)
        k_bf = sb.tile([P, N * PACK], BF16, name="k_bf", align_bytes=64)
        k_codes = sb.tile([P, N], U32, name="k_codes", align_bytes=64)
        k_scales = sb.tile([P, N], U8, name="k_scales", align_bytes=64)
        v_raw = sb.tile([P, KV, PACK, D], F32, name="v_raw", align_bytes=64)
        v_bf = sb.tile([P, KV * D * PACK], BF16, name="v_bf", align_bytes=64)
        v_codes = sb.tile([P, KV * D], U32, name="v_codes", align_bytes=64)
        v_scales = sb.tile([P, KV * D], U8, name="v_scales", align_bytes=64)
        t_sb = sb.tile([P, PACK], F32, name="t_sb", align_bytes=64)
        t_wide = sb.tile([P, QC * PACK], F32, name="t_wide", align_bytes=64)
        gn_sb = sb.tile([P, D], F32, name="gn_sb", align_bytes=64)
        og_sb = sb.tile([P, H, CHUNKS, D], F32, name="og_sb", align_bytes=64)
        gate = sb.tile([P, GROUPS, GW], F32, name="gate", align_bytes=64)
        p_sb = sb.tile([P, P_BUFS, GW * PACK], F32, name="p_sb", align_bytes=64)
        w_bf = sb.tile([P, GROUPS, GW * PACK], BF16, name="w_bf", align_bytes=64)
        w_codes = sb.tile([P, GROUPS, GW], U32, name="w_codes", align_bytes=64)
        w_scales = sb.tile([P, GROUPS, GW], U8, name="w_scales", align_bytes=64)
        squares = sb.tile([P, GROUPS, GW], BF16, name="squares", align_bytes=64)
        sums = sb.tile([P, GROUPS * TILES], F32, name="sums", align_bytes=64)
        factor = sb.tile([P, GROUPS * TILES], F32, name="factor", align_bytes=64)
        steps = sb.tile([P, 9, 16], F32, name="steps", align_bytes=64)
        warm = sb.tile([P, 2, 8], F32, name="warm", align_bytes=64)
        res = sb.tile([P, GROUPS, GW], F32, name="res", align_bytes=64)
        s_bank = [ps.tile([P, PACK * QC], F32, name="s_bank%d" % g) for g in range(TILES)]
        y_bank = [ps.tile([P, GW], F32, name="y_bank%d" % b) for b in range(Y_BANKS)]

        def load_k(i0, i1):
            both = kT.rearrange("k (p j) i -> (k p) j i", j=PACK)
            nc.sync.dma_start(out=k_raw[ROWS : 3 * ROWS, :, i0:i1], in_=both[:, :, i0:i1])
            nc.sync.dma_start(out=k_raw[0:ROWS, :, i0:i1], in_=both[0:ROWS, :, i0:i1])
            nc.scalar.dma_start(out=k_raw[3 * ROWS : P, :, i0:i1], in_=both[ROWS : 2 * ROWS, :, i0:i1])

        def load_q(hs, c0, c1):
            for g0, g1 in RUNS[hs]:
                h0 = HEADS[hs][g0]
                nc.sync.dma_start(
                    out=q_raw[ROWS * g0 : ROWS * g1, hs, :, c0 * QC : c1 * QC],
                    in_=qT[h0 : h0 + g1 - g0, :, c0 * QC : c1 * QC].rearrange("h (p j) q -> (h p) j q", j=PACK),
                )

        def load_og(hs):
            for g0 in (0, HALF):
                h0 = HEADS[hs][g0]
                nc.sync.dma_start(
                    out=og_sb[:, TILES * hs + g0 : TILES * hs + g0 + HALF, :, :].rearrange("p h c e -> p (h c) e"),
                    in_=og[h0 : h0 + HALF].rearrange("h (c p) e -> p (h c) e", p=P),
                )

        def quantize(codes, scales, source, c0, c1):
            nc.vector.quantize_mx(
                out=codes[:, c0:c1].bitcast(FP8X4), scales=scales[:, c0:c1], in_=source[:, c0 * PACK : c1 * PACK]
            )

        def cast_k(copy, s0, s1):
            copy(
                out=k_bf[:].rearrange("p (r s j) -> p s j r", r=PACK, j=PACK)[:, s0:s1, :, :],
                in_=k_raw[:].rearrange("p j (s r) -> p s j r", r=PACK)[:, s0:s1, :, :],
            )

        def cast_q(copy, hs, c0, c1):
            lo, hi = (hs * NQ + c0 * QC) * PACK, (hs * NQ + c1 * QC) * PACK
            copy(
                out=q_bf[:, lo:hi].rearrange("p (m c j) -> p m j c", c=LINE, j=PACK),
                in_=q_raw[:, hs, :, c0 * QC : c1 * QC].rearrange("p j (m c) -> p m j c", c=LINE),
            )

        def quantize_q(hs, c0, c1):
            quantize(q_codes, q_scales, q_bf, hs * NQ + c0 * QC, hs * NQ + c1 * QC)

        def scores(n):
            hs, c = divmod(n, CHUNKS)
            cols = slice(hs * NQ + c * QC, hs * NQ + (c + 1) * QC)
            for g in range(TILES):
                rows = slice(ROWS * g, ROWS * (g + 1))
                for r in range(PACK):
                    keys = slice(r * P, (r + 1) * P)
                    nc.tensor.matmul_mx(
                        out=s_bank[g][:, r * QC : (r + 1) * QC],
                        lhsT=k_codes[rows, keys].bitcast(FP8X4),
                        lhsT_scale=k_scales[rows, keys],
                        rhs=q_codes[rows, cols].bitcast(FP8X4),
                        rhs_scale=q_scales[rows, cols],
                        start=True,
                        stop=True,
                    )

        def silu(n, g0=0, g1=TILES):
            for g in range(g0, g1):
                nc.scalar.activation(
                    out=p_sb[:, n % P_BUFS, g * QC * PACK : (g + 1) * QC * PACK].rearrange("p (q r) -> p q r", r=PACK),
                    in_=s_bank[g][:].rearrange("p (r q) -> p q r", r=PACK),
                    func=ACT.Silu,
                )

        def weigh(n, half):
            lo, hi = half * HALF * QC * PACK, (half + 1) * HALF * QC * PACK
            nc.vector.tensor_tensor(
                out=w_bf[:, n, lo:hi].rearrange("p (g w) -> p g w", g=HALF),
                in0=p_sb[:, n % P_BUFS, lo:hi].rearrange("p (g w) -> p g w", g=HALF),
                in1=t_wide[:].unsqueeze(1).to_broadcast([P, HALF, QC * PACK]),
                op=ALU.mult,
            )

        def quantize_w(n, g0=0, g1=TILES):
            quantize(w_codes[:, n, :], w_scales[:, n, :], w_bf[:, n, :], g0 * QC, g1 * QC)

        def y_of(n, g):
            bank = n + 1 if n == LAST and g >= HALF else n
            return y_bank[bank % Y_BANKS][:, g * D : (g + 1) * D]

        def values(n, g0=0, g1=TILES):
            for g in range(g0, g1):
                cols = slice(g * QC, (g + 1) * QC)
                feats = slice((g // HALF) * D, (g // HALF + 1) * D)
                nc.tensor.matmul_mx(
                    out=y_of(n, g),
                    lhsT=w_codes[:, n, cols].bitcast(FP8X4),
                    lhsT_scale=w_scales[:, n, cols],
                    rhs=v_codes[:, feats].bitcast(FP8X4),
                    rhs_scale=v_scales[:, feats],
                    start=True,
                    stop=True,
                )

        def square(n, g0=0, g1=TILES):
            for g in range(g0, g1):
                nc.scalar.activation(
                    out=squares[:, n, g * D : (g + 1) * D],
                    in_=y_of(n, g),
                    func=ACT.Square,
                    accum_out=sums[:, n * TILES + g : n * TILES + g + 1],
                )

        def root(c0, c1):
            nc.scalar.activation(
                out=factor[:, c0:c1], in_=sums[:, c0:c1], func=ACT.Abs_reciprocal_sqrt, scale=FOLD / D, bias=FOLD * EPS
            )

        def refine(x, z, z_scale, scratch, dst):
            xz, u, poly = scratch
            return [
                lambda: nc.vector.tensor_tensor(out=xz, in0=x, in1=z, op=ALU.mult),
                lambda: nc.vector.scalar_tensor_tensor(
                    out=u, in0=xz, scalar=1.0 / z_scale**2, in1=z, op0=ALU.mult, op1=ALU.mult
                ),
                lambda: nc.vector.scalar_tensor_tensor(
                    out=poly, in0=u, scalar=-10.0 / 3.0, in1=u, op0=ALU.add, op1=ALU.mult
                ),
                lambda: nc.vector.scalar_tensor_tensor(out=dst, in0=poly, scalar=5.0, in1=z, op0=ALU.add, op1=ALU.mult),
            ]

        def early_factor_steps():
            cols = slice(0, EARLY * TILES)
            row = [steps[:, i, cols] for i in range(9)]
            x, guess, better = row[0], row[1], row[5]
            lift = FOLD * KAPPA**4
            return [
                lambda: nc.vector.tensor_scalar(
                    out=x, in0=sums[:, cols], scalar1=lift / D, scalar2=lift * EPS, op0=ALU.mult, op1=ALU.add
                ),
                lambda: nc.vector.tensor_scalar(
                    out=guess.bitcast(I32), in0=x.bitcast(I32), scalar1=-0.5, scalar2=SEED, op0=ALU.mult, op1=ALU.add
                ),
                *refine(x, guess, 1.0, row[2:5], better),
                *refine(x, better, KAPPA, row[6:9], factor[:, cols]),
            ]

        def tanh(n):
            hs, c = divmod(n, CHUNKS)
            nc.scalar.activation(
                out=gate[:, n : n + 2, :].rearrange("p c (g e) -> p c g e", g=TILES),
                in_=og_sb[:, TILES * hs : TILES * (hs + 1), c : c + 2, :].rearrange("p g c e -> p c g e"),
                func=ACT.Tanh,
                scale=0.5,
            )

        def gain(n):
            view = gate[:, n : n + 2, :].rearrange("p c (g e) -> p (c g) e", g=TILES)
            nc.vector.scalar_tensor_tensor(
                out=view,
                in0=view,
                scalar=1.0,
                in1=gn_sb[:].unsqueeze(1).to_broadcast([P, 2 * TILES, D]),
                op0=ALU.add,
                op1=ALU.mult,
            )

        def finish(n):
            hs, c = divmod(n, CHUNKS)
            for g0, g1 in RUNS[hs]:
                for g in range(g0, g1):
                    cols = slice(g * D, (g + 1) * D)
                    nc.vector.scalar_tensor_tensor(
                        out=res[:, n, cols],
                        in0=y_of(n, g),
                        scalar=factor[:, n * TILES + g : n * TILES + g + 1],
                        in1=gate[:, n, cols],
                        op0=ALU.mult,
                        op1=ALU.mult,
                    )
                h0 = HEADS[hs][g0]
                nc.sync.dma_start(
                    out=out[h0 : h0 + g1 - g0, c * QC : (c + 1) * QC, :].rearrange("h q e -> q h e"),
                    in_=res[:, n, g0 * D : g1 * D].rearrange("p (h e) -> p h e", e=D),
                )


        load_k(0, N // 2)
        load_k(N // 2, N)
        load_q(0, 0, 1)
        nc.sync.dma_start(out=t_sb[:], in_=t.rearrange("(p r) o -> p (r o)", r=PACK))
        nc.vector.memset(warm[:, 0, :], 0.0)
        nc.scalar.activation(out=warm[:, 1, :], in_=warm[:, 0, :], func=ACT.Silu)
        load_q(0, 1, 2)
        nc.sync.dma_start(
            out=v_raw[:].rearrange("p k r e -> p k (r e)"), in_=v.rearrange("k (p r) e -> p k (r e)", r=PACK)
        )
        load_q(0, 2, CHUNKS)
        load_q(1, 0, 2)
        load_og(0)
        nc.sync.dma_start(out=gn_sb[:], in_=gn)
        load_q(1, 2, CHUNKS)
        load_og(1)

        cast_k(on_vector, 0, K_HALF)
        cast_k(on_vector, K_HALF, K_SHARE)
        cast_k(on_scalar, K_SHARE, P)
        cast_q(on_scalar, 0, 0, 1)
        quantize(k_codes, k_scales, k_bf, 0, N // 2)
        quantize_q(0, 0, 1)
        quantize(k_codes, k_scales, k_bf, N // 2, N)
        scores(0)

        cast_q(on_scalar, 0, 1, 2)
        nc.vector.tensor_copy(
            out=t_wide[:].rearrange("p (q r) -> p q r", r=PACK),
            in_=t_sb[:].unsqueeze(1).to_broadcast([P, QC, PACK]),
        )
        quantize_q(0, 1, 2)
        for k in range(KV):
            nc.vector.tensor_copy(
                out=v_bf[:, k * D * PACK : (k + 1) * D * PACK].rearrange("p (m c r) -> p m r c", c=LINE, r=PACK),
                in_=v_raw[:, k, :, :].rearrange("p r (m c) -> p m r c", c=LINE),
            )
        silu(0)
        scores(1)
        cast_q(on_vector, 0, 2, 3)
        cast_q(on_scalar, 0, 3, CHUNKS)
        weigh(0, 0)
        quantize(v_codes, v_scales, v_bf, 0, KV * D)
        quantize_q(0, 2, CHUNKS)
        weigh(0, 1)

        silu(1)
        scores(2)
        weigh(1, 0)
        weigh(1, 1)
        silu(2)
        scores(3)
        cast_q(on_scalar, 1, 0, 2)
        quantize_w(0)
        values(0)
        weigh(2, 0)
        quantize_w(1)
        values(1)
        weigh(2, 1)
        quantize_q(1, 0, 2)
        silu(3)
        quantize_w(2)
        scores(4)
        values(2)
        tanh(0)
        for n in range(EARLY):
            square(n)
        weigh(3, 0)
        weigh(3, 1)
        gain(0)

        silu(4, 0, HALF)
        tanh(2)
        silu(4, HALF, TILES)
        scores(5)
        cast_q(on_scalar, 1, 2, CHUNKS)
        short = early_factor_steps()
        short[0]()
        between = [
            lambda: quantize_w(3),
            lambda: weigh(4, 0),
            lambda: gain(2),
            lambda: weigh(4, 1),
            lambda: quantize_q(1, 2, CHUNKS),
            lambda: quantize_w(4),
        ]
        for step, longer in zip(short[1:], between):
            step()
            longer()
        short[7]()
        silu(5)
        scores(6)
        silu(6)
        scores(LAST)
        values(3)
        silu(LAST)
        tanh(4)
        tanh(6)
        for half in range(2):
            weigh(5, half)
            short[8 + half]()

        weigh(6, 0)
        quantize_w(5)
        weigh(6, 1)
        finish(0)
        values(4)
        finish(1)
        values(5)
        finish(2)
        quantize_w(6)
        values(6)
        weigh(LAST, 0)
        weigh(LAST, 1)
        gain(4)

        for n in (3, 4):
            square(n)
            root(n * TILES, (n + 1) * TILES)
        square(5)
        square(6)
        root(5 * TILES, 6 * TILES)
        quantize_w(LAST, 0, HALF)
        finish(3)
        values(LAST, 0, HALF)
        quantize_w(LAST, HALF, TILES)
        finish(4)
        values(LAST, HALF, TILES)
        square(LAST, 0, HALF)
        root(6 * TILES, LAST * TILES + HALF)
        square(LAST, HALF, TILES)
        root(LAST * TILES + HALF, GROUPS * TILES)
        gain(6)
        for n in (5, 6, LAST):
            finish(n)
